import numpy as np
import ml_dtypes


def mxq(x, axis, fmt="e4m3"):
    dtype, down = {"e4m3": (ml_dtypes.float8_e4m3fn, 7), "e5m2": (ml_dtypes.float8_e5m2, 14)}[fmt]
    v = np.moveaxis(np.asarray(x, np.float32).astype(ml_dtypes.bfloat16).astype(np.float64), axis, -1)
    blocks = v.reshape(v.shape[:-1] + (-1, 32))
    amax = np.abs(blocks).max(-1, keepdims=True)
    byte = np.maximum(np.where(amax > 0, np.frexp(amax)[1] - 1 + 127, 0) - down, 1)
    scale = np.exp2(byte - 127.0)
    codes = (blocks / scale).astype(np.float32).astype(dtype).astype(np.float64)
    return np.moveaxis((codes * scale).reshape(v.shape), -1, axis)


WIDE = False


def mx_kscale(k):
    if not WIDE:
        return np.ones(k)
    levels = np.array([10, -10, 5, -5, 0])
    if k % 512:
        return np.exp2(np.random.permutation(np.resize(levels, k // 32))).repeat(32)
    a = np.empty((k // 512, 16))
    for p in range(k // 512):
        a[p, :8] = np.random.permutation(np.resize(levels, 8))
        for g in range(8):
            far = levels[np.abs(levels - a[p, g]) >= 10]
            a[p, g + 8] = far[np.random.randint(len(far))]
    return np.exp2(a.ravel()).repeat(32)


def f64(x):
    return np.asarray(x).astype(np.float64)


def striped(idx):
    return np.tile(idx.reshape(-1, 16).T, (8, 1)).astype(np.uint16)


def unstriped(offs):
    return offs[:16].T.reshape(-1).astype(np.int64)


E2M1 = np.array([0.0, 0.5, 1.0, 1.5, 2.0, 3.0, 4.0, 6.0, -0.0, -0.5, -1.0, -1.5, -2.0, -3.0, -4.0, -6.0])


def pack_weight(w, fmt):
    k, n = w.shape
    w = f64(np.asarray(w, np.float32).astype(ml_dtypes.bfloat16)).reshape(k // 32, 32, n)
    amax = np.abs(w).max(1)
    if fmt == "e4m3":
        byte = np.frexp(amax)[1] - 1 + 127 - 7
    else:
        mant, ex = np.frexp(amax / 6.0)
        byte = np.where(mant > 0.5, ex, ex - 1) + 127
    byte = np.clip(np.where(amax > 0, byte, 1), 1, 254)
    scaled = (w * np.exp2(127.0 - byte)[:, None, :]).reshape(k, n).astype(np.float32)
    by_word = np.ascontiguousarray(scaled.reshape(k // 512, 128, 4, n).transpose(0, 1, 3, 2))
    if fmt == "e4m3":
        words = by_word.astype(ml_dtypes.float8_e4m3fn).view(np.uint8)
    else:
        c = by_word.astype(ml_dtypes.float4_e2m1fn).view(np.uint8) & 0xF
        words = (c[..., 0::2] | (c[..., 1::2] << 4)).reshape(k // 512, 128, 2 * n)
    return np.ascontiguousarray(words), np.ascontiguousarray(byte.astype(np.uint8).reshape(k // 512, 16, n))


def unpack_weight(words, scales, fmt):
    g, _, n = scales.shape
    words = np.ascontiguousarray(words).reshape(g, 128, n, -1)
    if fmt == "e4m3":
        vals = words.view(ml_dtypes.float8_e4m3fn).astype(np.float64)
    else:
        nib = np.empty((g, 128, n, 4), np.uint8)
        nib[..., 0::2] = words & 0xF
        nib[..., 1::2] = words >> 4
        vals = E2M1[nib]
    vals = vals * np.repeat(np.exp2(scales.astype(np.float64) - 127.0), 8, axis=1)[..., None]
    return vals.transpose(0, 1, 3, 2).reshape(g * 512, n)


def gelu(v):
    return 0.5 * v * (1.0 + np.tanh(np.sqrt(2.0 / np.pi) * (v + 0.044715 * v**3)))


K, K2, T, S, H, N = 1024, 512, 4096, 1024, 1024, 512

def setup_inputs():
    n = np.random.standard_normal
    s = mx_kscale(K)[:, None]
    s2 = mx_kscale(K2)[:, None]
    u = mx_kscale(H)[:, None]
    d = {}
    d["tab_words"], d["tab_scales"] = pack_weight(n((K, T)) * s, "e4m3")
    d["offs"] = striped(np.random.permutation(T)[:S])
    d["xs_words"], d["xs_scales"] = pack_weight(n((K2, S)) * s2, "e4m3")
    d["w1"] = (1.5 * n((K, H)) / s / K ** 0.5).astype(np.float32)
    d["w2_words"], d["w2_scales"] = pack_weight(1.5 * n((K2, H)) / s2 / K2 ** 0.5, "e2m1")
    d["gain"] = (np.exp(0.3 * n(H)) * u[:, 0]).astype(np.float32)
    d["w3"] = (1.5 * n((H, N)) / u / H ** 0.5).astype(np.float32)
    return d

def reference(tab_words, tab_scales, offs, xs_words, xs_scales, w1, w2_words, w2_scales, gain, w3):
    v = unpack_weight(tab_words, tab_scales, "e4m3")[:, unstriped(offs)]
    xs = unpack_weight(xs_words, xs_scales, "e4m3")
    w2 = unpack_weight(w2_words, w2_scales, "e2m1")
    a = mxq(f64(w1), 0, "e4m3").T @ v
    b = w2.T @ xs
    size = 1.0 + (np.abs(a) + np.abs(b))
    h = f64(gain)[:, None] * ((a - b) / size)
    out = mxq(f64(w3), 0, "e4m3").T @ mxq(h, 0, "e4m3")
    return out

@@ -1,0 +1,305 @@
+from contextlib import ExitStack
+
+import concourse.mybir as mybir
+
+K, K2, T, S, H, N = 1024, 512, 4096, 1024, 1024, 512
+FLOPS = 2 * (K * H * S + K2 * H * S + H * N * S)
+BYTES = (K * T + K // 32 * T) + 2 * 128 * 64 + (K2 * S + K2 // 32 * S) + 4 * K * H + (K2 * H // 2 + K2 // 32 * H) + 4 * H + 4 * H * N + 4 * N * S
+
+F32 = mybir.dt.float32
+BF16 = mybir.dt.bfloat16
+I32 = mybir.dt.int32
+U32 = mybir.dt.uint32
+U16 = mybir.dt.uint16
+U8 = mybir.dt.uint8
+FP8X4 = mybir.dt.float8_e4m3fn_x4
+FP4X4 = mybir.dt.float4_e2m1fn_x4
+ALU = mybir.AluOpType
+ACT = mybir.ActivationFunctionType
+
+P = 128
+PACK = 4
+PASS = P * PACK
+BANK = 512
+HALF = 512
+GROUPS = [(0, 0, 512), (0, 512, 512), (1, 0, 512), (1, 512, 256), (1, 768, 128), (1, 896, 128)]
+
+
+def tile_list_sail_trim_contrast_kernel(tc, tab_words, tab_scales, offs, xs_words, xs_scales, w1, w2_words, w2_scales, gain, w3, out):
+    nc = tc.nc
+    with ExitStack() as ctx:
+        keep = ctx.enter_context(tc.tile_pool(name="keep", bufs=1))
+        raws = ctx.enter_context(tc.tile_pool(name="raws", bufs=6))
+        casts = ctx.enter_context(tc.tile_pool(name="casts", bufs=2))
+        ring = ctx.enter_context(tc.tile_pool(name="ring", bufs=4))
+        hring = ctx.enter_context(tc.tile_pool(name="hring", bufs=3))
+        psum_ab = ctx.enter_context(tc.psum_pool(name="psum_ab", bufs=6))
+        psum_o = ctx.enter_context(tc.psum_pool(name="psum_o", bufs=2))
+
+        offsets = keep.tile([P, S // 16], U16, name="offsets")
+        tabw = [keep.tile([P, T], I32, name=f"tabw{a}", align_bytes=64) for a in range(2)]
+        tabs = keep.tile([P, T], U8, name="tabs", align_bytes=64)
+        xsw = keep.tile([P, S], I32, name="xsw", align_bytes=64)
+        xss = keep.tile([P, S], U8, name="xss", align_bytes=64)
+        w2w = keep.tile([P, 2 * H], U8, name="w2w", align_bytes=64)
+        w2s = keep.tile([P, H], U8, name="w2s", align_bytes=64)
+        w2w_dealt = [keep.tile([P, 2 * PASS], U8, name=f"w2wd{b}", align_bytes=64) for b in range(2)]
+        w2s_dealt = [keep.tile([P, PASS], U8, name=f"w2sd{b}", align_bytes=64) for b in range(2)]
+        gains = keep.tile([P, 2, PACK], F32, name="gains")
+        warm = keep.tile([P, 8], F32, name="warm")
+        vw = [[keep.tile([P, HALF], U32, name=f"vw{a}{jh}", align_bytes=64) for jh in range(2)] for a in range(2)]
+        vs = [keep.tile([P, HALF], U8, name=f"vs{jh}", align_bytes=64) for jh in range(2)]
+        w1w = [[keep.tile([P, PASS], U32, name=f"w1w{a}{b}", align_bytes=64) for b in range(2)] for a in range(2)]
+        w1s = [[keep.tile([P, PASS], U8, name=f"w1s{a}{b}", align_bytes=64) for b in range(2)] for a in range(2)]
+        w3w = [keep.tile([P, N], U32, name=f"w3w{b}", align_bytes=64) for b in range(2)]
+        w3s = [keep.tile([P, N], U8, name=f"w3s{b}", align_bytes=64) for b in range(2)]
+        hw = [[keep.tile([P, HALF], U32, name=f"hw{b}{jh}", align_bytes=64) for jh in range(2)] for b in range(2)]
+        hs = [[keep.tile([P, HALF], U8, name=f"hs{b}{jh}", align_bytes=64) for jh in range(2)] for b in range(2)]
+        num = [[keep.tile([P, PACK, HALF], F32, name=f"num{b}{jh}", align_bytes=64) for jh in range(2)] for b in range(2)]
+        den = [[keep.tile([P, PACK, HALF], F32, name=f"den{b}{jh}", align_bytes=64) for jh in range(2)] for b in range(2)]
+
+        nc.gpsimd.memset(w2s[:].bitcast(I32), 0)
+        nc.gpsimd.memset(xss[:].bitcast(I32), 0)
+        nc.vector.memset(warm[:], 1.0)
+        nc.vector.memset(tabs[:].bitcast(I32), 0)
+        nc.scalar.activation(warm[:], warm[:], ACT.Abs_reciprocal_sqrt, bias=1.0)
+
+        nc.sync.dma_start(w2w[:].bitcast(I32), w2_words[0].bitcast(I32))
+        nc.sync.dma_start(offsets[:], offs)
+        for q in range(4):
+            nc.sync.dma_start(w2s[32 * q : 32 * q + 4, :].bitcast(I32), w2_scales[0, 4 * q : 4 * q + 4, :].bitcast(I32))
+        nc.sync.dma_start(xsw[:], xs_words[0].rearrange("p c i -> p (c i)").bitcast(I32))
+        for q in range(4):
+            nc.sync.dma_start(xss[32 * q : 32 * q + 4, :].bitcast(I32), xs_scales[0, 4 * q : 4 * q + 4, :].bitcast(I32))
+
+        w1_raw = {}
+        w3_raw = {}
+
+        def load_w1(a, b):
+            w1_raw[a, b] = raws.tile([P, PACK, PASS], F32, name="raw")
+            rows = w1[PASS * a : PASS * (a + 1), PASS * b : PASS * (b + 1)]
+            nc.sync.dma_start(w1_raw[a, b][:], rows.rearrange("(p i) c -> p i c", i=PACK))
+
+        def load_w3(b):
+            w3_raw[b] = raws.tile([P, PACK, N], F32, name="raw")
+            nc.sync.dma_start(w3_raw[b][:], w3[PASS * b : PASS * (b + 1), :].rearrange("(p i) c -> p i c", i=PACK))
+
+        load_w1(0, 0)
+        nc.sync.dma_start(gains[:], gain.rearrange("(b p t) -> p b t", b=2, t=PACK))
+        load_w1(1, 0)
+        nc.sync.dma_start(tabw[0][:], tab_words[0].rearrange("p t i -> p (t i)").bitcast(I32))
+        for q in range(4):
+            nc.sync.dma_start(tabs[32 * q : 32 * q + 8, :].bitcast(I32), tab_scales[:, 4 * q : 4 * q + 4, :].bitcast(I32))
+        nc.sync.dma_start(tabw[1][:], tab_words[1].rearrange("p t i -> p (t i)").bitcast(I32))
+        load_w1(0, 1)
+        load_w1(1, 1)
+        load_w3(0)
+        load_w3(1)
+
+        def deal_w2(b):
+            nc.vector.tensor_copy(
+                w2w_dealt[b][:].rearrange("p (t m y) -> p t m y", t=PACK, y=2),
+                w2w[:, 2 * PASS * b : 2 * PASS * (b + 1)].rearrange("p (m t y) -> p t m y", t=PACK, y=2),
+            )
+            nc.vector.tensor_copy(
+                w2s_dealt[b][:].rearrange("p (t m) -> p t m", t=PACK),
+                w2s[:, PASS * b : PASS * (b + 1)].rearrange("p (m t) -> p t m", t=PACK),
+            )
+
+        def sensors(b, jh):
+            cols = slice(HALF * jh, HALF * (jh + 1))
+            for t in range(PACK):
+                bank = psum_ab.tile([P, BANK], F32, name="bank_ab")
+                nc.tensor.matmul_mx(
+                    out=bank[:],
+                    lhsT=w2w_dealt[b][:, 2 * P * t : 2 * P * (t + 1)].bitcast(FP4X4),
+                    lhsT_scale=w2s_dealt[b][:, P * t : P * (t + 1)],
+                    rhs=xsw[:, cols].bitcast(FP8X4),
+                    rhs_scale=xss[:, cols],
+                    start=True,
+                    stop=True,
+                )
+                nc.scalar.activation(den[b][jh][:, t, :], bank[:], ACT.Abs)
+                if t % 2 == 0:
+                    nc.scalar.activation(num[b][jh][:, t, :], bank[:], ACT.Copy, scale=gains[:, b, t : t + 1])
+                else:
+                    nc.vector.tensor_scalar_mul(num[b][jh][:, t, :], bank[:], gains[:, b, t : t + 1])
+
+        rounded = {}
+
+        def round_w1(a, b):
+            rounded["w1", a, b] = casts.tile([P, PASS * PACK], BF16, name="rounded", align_bytes=64)
+            nc.vector.tensor_copy(
+                rounded["w1", a, b][:].rearrange("p (t m i) -> p m i t", t=PACK, i=PACK),
+                w1_raw[a, b][:].rearrange("p i (m t) -> p m i t", t=PACK),
+            )
+
+        def quantise_w1(a, b):
+            nc.vector.quantize_mx(out=w1w[a][b][:].bitcast(FP8X4), scales=w1s[a][b][:], in_=rounded["w1", a, b][:])
+
+        def round_w3(b):
+            rounded["w3", b] = casts.tile([P, N * PACK], BF16, name="rounded", align_bytes=64)
+            nc.scalar.copy(
+                rounded["w3", b][:].rearrange("p (c e i) -> p c i e", e=4, i=PACK),
+                w3_raw[b][:].rearrange("p i (c e) -> p c i e", e=4),
+            )
+
+        def quantise_w3(b):
+            nc.vector.quantize_mx(out=w3w[b][:].bitcast(FP8X4), scales=w3s[b][:], in_=rounded["w3", b][:])
+
+        def part_of_list(jh):
+            return offsets[:, HALF // 16 * jh : HALF // 16 * (jh + 1)]
+
+        def gather_words(a, jh):
+            nc.vector.tensor_copy(vw[a][jh][:], tabw[a][:].bitcast(U32).indirect(part_of_list(jh)))
+
+        def gather_scales(jh):
+            nc.vector.tensor_copy(vs[jh][:], tabs[:].indirect(part_of_list(jh)))
+
+        units = []
+        for b, j0, width in GROUPS:
+            nt = BANK // width
+            for t0 in range(0, PACK, nt):
+                units.append((b, j0, width, t0, nt))
+        banks = {}
+        mags = {}
+
+        def view(tiles, u):
+            b, j0, width, t0, nt = units[u]
+            return tiles[b][j0 // HALF][:, t0 : t0 + nt, j0 % HALF : j0 % HALF + width]
+
+        def shapes(u):
+            b, j0, width, t0, nt = units[u]
+            jh = j0 // HALF
+            cols = slice(j0 % HALF, j0 % HALF + width)
+            banks[u] = psum_ab.tile([P, nt, width], F32, name="bank_ab")
+            for t in range(t0, t0 + nt):
+                for a in range(2):
+                    nc.tensor.matmul_mx(
+                        out=banks[u][:, t - t0, :],
+                        lhsT=w1w[a][b][:, P * t : P * (t + 1)].bitcast(FP8X4),
+                        lhsT_scale=w1s[a][b][:, P * t : P * (t + 1)],
+                        rhs=vw[a][jh][:, cols].bitcast(FP8X4),
+                        rhs_scale=vs[jh][4 * a :, cols],
+                        start=(a == 0),
+                        stop=(a == 1),
+                    )
+
+        def magnitude(u):
+            b, j0, width, t0, nt = units[u]
+            mags[u] = ring.tile([P, nt, width], F32, name="mag")
+            nc.scalar.activation(mags[u][:], banks[u][:], ACT.Abs)
+
+        def numerator(u):
+            b, j0, width, t0, nt = units[u]
+            for t in range(nt):
+                part = view(num, u)[:, t, :]
+                nc.vector.scalar_tensor_tensor(part, banks[u][:, t, :], gains[:, b, t0 + t : t0 + t + 1], part, ALU.mult, ALU.subtract)
+
+        def both_sizes(u):
+            nc.vector.tensor_tensor(view(den, u), mags[u][:], view(den, u), ALU.add)
+
+        def inverse_root(u):
+            nc.scalar.activation(view(den, u), view(den, u), ACT.Abs_reciprocal_sqrt, bias=1.0)
+
+        def inverse(u):
+            nc.scalar.activation(view(den, u), view(den, u), ACT.Square)
+
+        h_rounded = {}
+
+        def contrast(b, j0, width):
+            jh = j0 // HALF
+            cols = slice(j0 % HALF, j0 % HALF + width)
+            h_rounded[b, j0] = hring.tile([P, width * PACK], BF16, name="h_rounded", align_bytes=64)
+            nc.vector.tensor_tensor(
+                h_rounded[b, j0][:].rearrange("p (c e t) -> p c t e", e=2, t=PACK),
+                num[b][jh][:, :, cols].rearrange("p t (c e) -> p c t e", e=2),
+                den[b][jh][:, :, cols].rearrange("p t (c e) -> p c t e", e=2),
+                ALU.mult,
+            )
+
+        def quantise_h(b, j0, width):
+            jh = j0 // HALF
+            cols = slice(j0 % HALF, j0 % HALF + width)
+            nc.vector.quantize_mx(out=hw[b][jh][:, cols].bitcast(FP8X4), scales=hs[b][jh][:, cols], in_=h_rounded[b, j0][:])
+
+        out_rows = out.rearrange("(n p) j -> p n j", p=P)
+
+        def features(j0, width):
+            jh = j0 // HALF
+            cols = slice(j0 % HALF, j0 % HALF + width)
+            nn = BANK // width
+            for n0 in range(0, N // P, nn):
+                bank = psum_o.tile([P, nn, width], F32, name="bank_o")
+                for n in range(n0, n0 + nn):
+                    for b in range(2):
+                        nc.tensor.matmul_mx(
+                            out=bank[:, n - n0, :],
+                            lhsT=w3w[b][:, P * n : P * (n + 1)].bitcast(FP8X4),
+                            lhsT_scale=w3s[b][:, P * n : P * (n + 1)],
+                            rhs=hw[b][jh][:, cols].bitcast(FP8X4),
+                            rhs_scale=hs[b][jh][:, cols],
+                            start=(b == 0),
+                            stop=(b == 1),
+                        )
+                staged = ring.tile([P, nn, width], F32, name="staged")
+                if width == BANK:
+                    nc.scalar.copy(staged[:], bank[:])
+                else:
+                    nc.vector.tensor_copy(staged[:], bank[:])
+                nc.sync.dma_start(out_rows[:, n0 : n0 + nn, j0 : j0 + width], staged[:])
+
+        deal_w2(0)
+        sensors(0, 0)
+        deal_w2(1)
+        round_w1(0, 0)
+        sensors(0, 1)
+        round_w1(1, 0)
+        quantise_w1(0, 0)
+        gather_scales(0)
+        quantise_w1(1, 0)
+        gather_words(0, 0)
+        gather_scales(1)
+        gather_words(0, 1)
+        sensors(1, 0)
+        sensors(1, 1)
+        gather_words(1, 0)
+
+        later = {
+            0: [lambda: gather_words(1, 1)],
+            1: [lambda: round_w1(0, 1)],
+            2: [lambda: quantise_w1(0, 1)],
+            3: [lambda: round_w1(1, 1)],
+            4: [lambda: quantise_w1(1, 1)],
+            5: [lambda: round_w3(0)],
+            6: [lambda: quantise_w3(0)],
+            7: [lambda: round_w3(1)],
+            8: [lambda: quantise_w3(1)],
+        }
+
+        def after(step, work):
+            later.setdefault(step, []).append(work)
+
+        shapes(0)
+        for step in range(len(units) + 8):
+            if step + 1 < len(units):
+                shapes(step + 1)
+            if step < len(units):
+                magnitude(step)
+            if 0 <= step - 1 < len(units):
+                both_sizes(step - 1)
+                numerator(step - 1)
+            if 0 <= step - 2 < len(units):
+                inverse(step - 2)
+                b, j0, width, t0, nt = units[step - 2]
+                if t0 + nt == PACK:
+                    piece = min(width, 256)
+                    for n, c0 in enumerate(range(j0, j0 + width, piece)):
+                        after(step + 1 + n, lambda b=b, c0=c0, piece=piece: contrast(b, c0, piece))
+                        after(step + 2 + n, lambda b=b, c0=c0, piece=piece: quantise_h(b, c0, piece))
+                    if b == 1:
+                        after(step + 1 + width // piece, lambda j0=j0, width=width: features(j0, width))
+            if 0 <= step - 1 < len(units):
+                inverse_root(step - 1)
+            for work in later.get(step, []):
+                work()

@@ -1,6 +1,7 @@
 from contextlib import ExitStack
 
 import concourse.mybir as mybir
+from concourse.masks import make_identity
 
 K, K2, T, S, H, N = 1024, 512, 4096, 1024, 1024, 512
 FLOPS = 2 * (K * H * S + K2 * H * S + H * N * S)
@@ -23,6 +24,12 @@ PASS = P * PACK
 BANK = 512
 HALF = 512
 GROUPS = [(0, 0, 512), (0, 512, 512), (1, 0, 512), (1, 512, 256), (1, 768, 128), (1, 896, 128)]
+H1V = [(0, 0, 0), (0, 0, 1), (0, 0, 2), (0, 0, 3), (0, 1, 0), (0, 1, 1), (0, 1, 2), (0, 1, 3)]
+CAST = "vvvvvv"
+MODE = "ppppppppppppppss"
+M6 = "ppppvv"
+OUTE = "ssssssss"
+PIECE = [256,256,256,256,128,128]
 
 
 def tile_list_sail_trim_contrast_kernel(tc, tab_words, tab_scales, offs, xs_words, xs_scales, w1, w2_words, w2_scales, gain, w3, out):
@@ -33,7 +40,8 @@ def tile_list_sail_trim_contrast_kernel(tc, tab_words, tab_scales, offs, xs_word
         casts = ctx.enter_context(tc.tile_pool(name="casts", bufs=2))
         ring = ctx.enter_context(tc.tile_pool(name="ring", bufs=4))
         hring = ctx.enter_context(tc.tile_pool(name="hring", bufs=3))
-        psum_ab = ctx.enter_context(tc.psum_pool(name="psum_ab", bufs=6))
+        psum_ab = ctx.enter_context(tc.psum_pool(name="psum_ab", bufs=4))
+        psum_x = ctx.enter_context(tc.psum_pool(name="psum_x", bufs=2))
         psum_o = ctx.enter_context(tc.psum_pool(name="psum_o", bufs=2))
 
         offsets = keep.tile([P, S // 16], U16, name="offsets")
@@ -60,17 +68,11 @@ def tile_list_sail_trim_contrast_kernel(tc, tab_words, tab_scales, offs, xs_word
 
         nc.gpsimd.memset(w2s[:].bitcast(I32), 0)
         nc.gpsimd.memset(xss[:].bitcast(I32), 0)
+        identity = keep.tile([P, P], F32, name="identity")
+        make_identity(nc, identity[:])
         nc.vector.memset(warm[:], 1.0)
         nc.vector.memset(tabs[:].bitcast(I32), 0)
         nc.scalar.activation(warm[:], warm[:], ACT.Abs_reciprocal_sqrt, bias=1.0)
-
-        nc.sync.dma_start(w2w[:].bitcast(I32), w2_words[0].bitcast(I32))
-        nc.sync.dma_start(offsets[:], offs)
-        for q in range(4):
-            nc.sync.dma_start(w2s[32 * q : 32 * q + 4, :].bitcast(I32), w2_scales[0, 4 * q : 4 * q + 4, :].bitcast(I32))
-        nc.sync.dma_start(xsw[:], xs_words[0].rearrange("p c i -> p (c i)").bitcast(I32))
-        for q in range(4):
-            nc.sync.dma_start(xss[32 * q : 32 * q + 4, :].bitcast(I32), xs_scales[0, 4 * q : 4 * q + 4, :].bitcast(I32))
 
         w1_raw = {}
         w3_raw = {}
@@ -84,12 +86,19 @@ def tile_list_sail_trim_contrast_kernel(tc, tab_words, tab_scales, offs, xs_word
             w3_raw[b] = raws.tile([P, PACK, N], F32, name="raw")
             nc.sync.dma_start(w3_raw[b][:], w3[PASS * b : PASS * (b + 1), :].rearrange("(p i) c -> p i c", i=PACK))
 
+        nc.sync.dma_start(w2w[:].bitcast(I32), w2_words[0].bitcast(I32))
+        nc.sync.dma_start(xsw[:], xs_words[0].rearrange("p c i -> p (c i)").bitcast(I32))
+        nc.sync.dma_start(offsets[:], offs)
+        for q in range(4):
+            nc.sync.dma_start(w2s[32 * q : 32 * q + 4, :].bitcast(I32), w2_scales[0, 4 * q : 4 * q + 4, :].bitcast(I32))
         load_w1(0, 0)
+        for q in range(4):
+            nc.sync.dma_start(xss[32 * q : 32 * q + 4, :].bitcast(I32), xs_scales[0, 4 * q : 4 * q + 4, :].bitcast(I32))
         nc.sync.dma_start(gains[:], gain.rearrange("(b p t) -> p b t", b=2, t=PACK))
         load_w1(1, 0)
-        nc.sync.dma_start(tabw[0][:], tab_words[0].rearrange("p t i -> p (t i)").bitcast(I32))
         for q in range(4):
             nc.sync.dma_start(tabs[32 * q : 32 * q + 8, :].bitcast(I32), tab_scales[:, 4 * q : 4 * q + 4, :].bitcast(I32))
+        nc.sync.dma_start(tabw[0][:], tab_words[0].rearrange("p t i -> p (t i)").bitcast(I32))
         nc.sync.dma_start(tabw[1][:], tab_words[1].rearrange("p t i -> p (t i)").bitcast(I32))
         load_w1(0, 1)
         load_w1(1, 1)
@@ -98,18 +107,19 @@ def tile_list_sail_trim_contrast_kernel(tc, tab_words, tab_scales, offs, xs_word
 
         def deal_w2(b):
             nc.vector.tensor_copy(
-                w2w_dealt[b][:].rearrange("p (t m y) -> p t m y", t=PACK, y=2),
-                w2w[:, 2 * PASS * b : 2 * PASS * (b + 1)].rearrange("p (m t y) -> p t m y", t=PACK, y=2),
+                w2w_dealt[b][:].bitcast(U16).rearrange("p (t m) -> p t m", t=PACK),
+                w2w[:, 2 * PASS * b : 2 * PASS * (b + 1)].bitcast(U16).rearrange("p (m t) -> p t m", t=PACK),
             )
             nc.vector.tensor_copy(
                 w2s_dealt[b][:].rearrange("p (t m) -> p t m", t=PACK),
                 w2s[:, PASS * b : PASS * (b + 1)].rearrange("p (m t) -> p t m", t=PACK),
             )
 
-        def sensors(b, jh):
+        def sensors(b, jh, ts=range(PACK)):
             cols = slice(HALF * jh, HALF * (jh + 1))
-            for t in range(PACK):
-                bank = psum_ab.tile([P, BANK], F32, name="bank_ab")
+            for t in ts:
+                pool, tag = [(psum_o, "bank_o"), (psum_x, "bank_x"), (psum_ab, "bank_ab"), (psum_o, "bank_o")][t]
+                bank = pool.tile([P, BANK], F32, name=tag)
                 nc.tensor.matmul_mx(
                     out=bank[:],
                     lhsT=w2w_dealt[b][:, 2 * P * t : 2 * P * (t + 1)].bitcast(FP4X4),
@@ -119,29 +129,39 @@ def tile_list_sail_trim_contrast_kernel(tc, tab_words, tab_scales, offs, xs_word
                     start=True,
                     stop=True,
                 )
-                nc.scalar.activation(den[b][jh][:, t, :], bank[:], ACT.Abs)
-                if t % 2 == 0:
-                    nc.scalar.activation(num[b][jh][:, t, :], bank[:], ACT.Copy, scale=gains[:, b, t : t + 1])
-                else:
+                nc.scalar.activation(den[b][jh][:, t, :], bank[:], ACT.Abs, scale=0.5)
+                if (b, jh, t) in H1V:
                     nc.vector.tensor_scalar_mul(num[b][jh][:, t, :], bank[:], gains[:, b, t : t + 1])
+                else:
+                    nc.scalar.activation(num[b][jh][:, t, :], bank[:], ACT.Copy, scale=gains[:, b, t : t + 1])
 
         rounded = {}
 
-        def round_w1(a, b):
-            rounded["w1", a, b] = casts.tile([P, PASS * PACK], BF16, name="rounded", align_bytes=64)
-            nc.vector.tensor_copy(
-                rounded["w1", a, b][:].rearrange("p (t m i) -> p m i t", t=PACK, i=PACK),
-                w1_raw[a, b][:].rearrange("p i (m t) -> p m i t", t=PACK),
+        def caster(which):
+            if which == "g":
+                return lambda dst, src: nc.gpsimd.tensor_scalar(dst, src, 1.0, 0.0, ALU.mult, ALU.add)
+            return nc.vector.tensor_copy if which == "v" else nc.scalar.copy
+
+        def round_w1(a, b, part=0, parts=1):
+            if part == 0:
+                pool, tag = (casts, "rounded") if b == 0 else (keep, "tabw1")
+                rounded["w1", a, b] = pool.tile([P, PASS * PACK], BF16, name=tag, align_bytes=64)
+            ms = slice(P // parts * part, P // parts * (part + 1))
+            caster(CAST[2 * b + a])(
+                rounded["w1", a, b][:].rearrange("p (t m i) -> p m i t", t=PACK, i=PACK)[:, ms],
+                w1_raw[a, b][:].rearrange("p i (m t) -> p m i t", t=PACK)[:, ms],
             )
 
         def quantise_w1(a, b):
             nc.vector.quantize_mx(out=w1w[a][b][:].bitcast(FP8X4), scales=w1s[a][b][:], in_=rounded["w1", a, b][:])
 
-        def round_w3(b):
-            rounded["w3", b] = casts.tile([P, N * PACK], BF16, name="rounded", align_bytes=64)
-            nc.scalar.copy(
-                rounded["w3", b][:].rearrange("p (c e i) -> p c i e", e=4, i=PACK),
-                w3_raw[b][:].rearrange("p i (c e) -> p c i e", e=4),
+        def round_w3(b, part=0, parts=1):
+            if part == 0:
+                rounded["w3", b] = keep.tile([P, N * PACK], BF16, name="tabw1", align_bytes=64)
+            cs = slice(P // parts * part, P // parts * (part + 1))
+            caster(CAST[4 + b])(
+                rounded["w3", b][:].rearrange("p (c e i) -> p c i e", e=4, i=PACK)[:, cs],
+                w3_raw[b][:].rearrange("p i (c e) -> p c i e", e=4)[:, cs],
             )
 
         def quantise_w3(b):
@@ -162,7 +182,6 @@ def tile_list_sail_trim_contrast_kernel(tc, tab_words, tab_scales, offs, xs_word
             for t0 in range(0, PACK, nt):
                 units.append((b, j0, width, t0, nt))
         banks = {}
-        mags = {}
 
         def view(tiles, u):
             b, j0, width, t0, nt = units[u]
@@ -185,10 +204,16 @@ def tile_list_sail_trim_contrast_kernel(tc, tab_words, tab_scales, offs, xs_word
                         stop=(a == 1),
                     )
 
-        def magnitude(u):
-            b, j0, width, t0, nt = units[u]
-            mags[u] = ring.tile([P, nt, width], F32, name="mag")
-            nc.scalar.activation(mags[u][:], banks[u][:], ACT.Abs)
+        mags = {}
+        sums = {}
+
+        def positive_part(u):
+            if MODE[u] == "v":
+                nc.vector.scalar_tensor_tensor(view(den, u), banks[u][:], 0.0, view(den, u), ALU.max, ALU.add)
+            else:
+                b, j0, width, t0, nt = units[u]
+                mags[u] = ring.tile([P, nt, width], F32, name="mag")
+                nc.scalar.activation(mags[u][:], banks[u][:], ACT.Abs, scale=0.5)
 
         def numerator(u):
             b, j0, width, t0, nt = units[u]
@@ -197,40 +222,65 @@ def tile_list_sail_trim_contrast_kernel(tc, tab_words, tab_scales, offs, xs_word
                 nc.vector.scalar_tensor_tensor(part, banks[u][:, t, :], gains[:, b, t0 + t : t0 + t + 1], part, ALU.mult, ALU.subtract)
 
         def both_sizes(u):
-            nc.vector.tensor_tensor(view(den, u), mags[u][:], view(den, u), ALU.add)
+            if MODE[u] == "v":
+                nc.vector.scalar_tensor_tensor(view(den, u), banks[u][:], -0.5, view(den, u), ALU.mult, ALU.add)
+            elif MODE[u] == "p":
+                b, j0, width, t0, nt = units[u]
+                sums[u] = psum_x.tile([P, nt, width], F32, name="bank_x")
+                for t in range(nt):
+                    for c0 in range(0, width, P):
+                        block = slice(c0, c0 + P)
+                        nc.tensor.matmul(sums[u][:, t, block], view(den, u)[:, t, block], identity[:], start=True, stop=False, is_transpose=True)
+                        nc.tensor.matmul(sums[u][:, t, block], mags[u][:, t, block], identity[:], start=False, stop=True, is_transpose=True)
+            else:
+                engine = nc.vector if MODE[u] == "s" else nc.gpsimd
+                engine.tensor_tensor(view(den, u), mags[u][:], view(den, u), ALU.add)
 
         def inverse_root(u):
-            nc.scalar.activation(view(den, u), view(den, u), ACT.Abs_reciprocal_sqrt, bias=1.0)
+            size = sums[u][:] if MODE[u] == "p" else view(den, u)
+            nc.scalar.activation(view(den, u), size, ACT.Abs_reciprocal_sqrt, bias=1.0, scale=2.0)
 
         def inverse(u):
             nc.scalar.activation(view(den, u), view(den, u), ACT.Square)
 
         h_rounded = {}
 
-        def contrast(b, j0, width):
+        def contrast(g, b, j0, width):
             jh = j0 // HALF
-            cols = slice(j0 % HALF, j0 % HALF + width)
-            h_rounded[b, j0] = hring.tile([P, width * PACK], BF16, name="h_rounded", align_bytes=64)
-            nc.vector.tensor_tensor(
-                h_rounded[b, j0][:].rearrange("p (c e t) -> p c t e", e=2, t=PACK),
-                num[b][jh][:, :, cols].rearrange("p t (c e) -> p c t e", e=2),
-                den[b][jh][:, :, cols].rearrange("p t (c e) -> p c t e", e=2),
-                ALU.mult,
-            )
+            h_rounded[b, j0] = hring.tile([P, width, PACK], BF16, name="h_rounded", align_bytes=64)
+            step = P if M6[g] == "p" else width
+            for c0 in range(0, width, step):
+                cols = slice(j0 % HALF + c0, j0 % HALF + c0 + step)
+                if M6[g] == "p":
+                    back = psum_o.tile([P, PACK, P], F32, name="bank_o")
+                    for t in range(PACK):
+                        nc.tensor.transpose(back[:, t, :], den[b][jh][:, t, cols], identity[:])
+                    inverses = back[:]
+                else:
+                    inverses = den[b][jh][:, :, cols]
+                nc.vector.tensor_tensor(
+                    h_rounded[b, j0][:, c0 : c0 + step, :].rearrange("p (c e) t -> p c t e", e=2),
+                    inverses.rearrange("p t (c e) -> p c t e", e=2),
+                    num[b][jh][:, :, cols].rearrange("p t (c e) -> p c t e", e=2),
+                    ALU.mult,
+                )
 
         def quantise_h(b, j0, width):
             jh = j0 // HALF
             cols = slice(j0 % HALF, j0 % HALF + width)
-            nc.vector.quantize_mx(out=hw[b][jh][:, cols].bitcast(FP8X4), scales=hs[b][jh][:, cols], in_=h_rounded[b, j0][:])
+            nc.vector.quantize_mx(out=hw[b][jh][:, cols].bitcast(FP8X4), scales=hs[b][jh][:, cols], in_=h_rounded[b, j0][:].rearrange("p c t -> p (c t)"))
 
         out_rows = out.rearrange("(n p) j -> p n j", p=P)
+
+        stored = []
 
         def features(j0, width):
             jh = j0 // HALF
             cols = slice(j0 % HALF, j0 % HALF + width)
             nn = BANK // width
             for n0 in range(0, N // P, nn):
-                bank = psum_o.tile([P, nn, width], F32, name="bank_o")
+                pool, tag = {"a": (psum_ab, "bank_ab"), "x": (psum_x, "bank_x"), "o": (psum_o, "bank_o")}["aaaaaaaa"[len(stored)]]
+                bank = pool.tile([P, nn, width], F32, name=tag)
                 for n in range(n0, n0 + nn):
                     for b in range(2):
                         nc.tensor.matmul_mx(
@@ -243,7 +293,8 @@ def tile_list_sail_trim_contrast_kernel(tc, tab_words, tab_scales, offs, xs_word
                             stop=(b == 1),
                         )
                 staged = ring.tile([P, nn, width], F32, name="staged")
-                if width == BANK:
+                stored.append(n0)
+                if OUTE[len(stored) - 1] == "s":
                     nc.scalar.copy(staged[:], bank[:])
                 else:
                     nc.vector.tensor_copy(staged[:], bank[:])
@@ -253,52 +304,54 @@ def tile_list_sail_trim_contrast_kernel(tc, tab_words, tab_scales, offs, xs_word
         sensors(0, 0)
         deal_w2(1)
         round_w1(0, 0)
-        sensors(0, 1)
         round_w1(1, 0)
         quantise_w1(0, 0)
-        gather_scales(0)
         quantise_w1(1, 0)
+        gather_scales(0)
         gather_words(0, 0)
+        gather_words(1, 0)
+        sensors(0, 1)
         gather_scales(1)
         gather_words(0, 1)
         sensors(1, 0)
         sensors(1, 1)
-        gather_words(1, 0)
 
         later = {
             0: [lambda: gather_words(1, 1)],
-            1: [lambda: round_w1(0, 1)],
-            2: [lambda: quantise_w1(0, 1)],
-            3: [lambda: round_w1(1, 1)],
-            4: [lambda: quantise_w1(1, 1)],
-            5: [lambda: round_w3(0)],
-            6: [lambda: quantise_w3(0)],
-            7: [lambda: round_w3(1)],
-            8: [lambda: quantise_w3(1)],
+            2: [lambda: round_w1(0, 1)],
+            3: [lambda: quantise_w1(0, 1)],
+            4: [lambda: round_w1(1, 1)],
+            5: [lambda: quantise_w1(1, 1)],
+            6: [lambda: round_w3(0)],
+            7: [lambda: quantise_w3(0)],
+            8: [lambda: round_w3(1)],
+            9: [lambda: quantise_w3(1)],
         }
 
         def after(step, work):
             later.setdefault(step, []).append(work)
 
         shapes(0)
-        for step in range(len(units) + 8):
-            if step + 1 < len(units):
-                shapes(step + 1)
+        shapes(1)
+        for step in range(len(units) + 10):
+            if step + 2 < len(units):
+                shapes(step + 2)
             if step < len(units):
-                magnitude(step)
+                positive_part(step)
             if 0 <= step - 1 < len(units):
-                both_sizes(step - 1)
                 numerator(step - 1)
+                both_sizes(step - 1)
             if 0 <= step - 2 < len(units):
                 inverse(step - 2)
                 b, j0, width, t0, nt = units[step - 2]
                 if t0 + nt == PACK:
-                    piece = min(width, 256)
+                    g = GROUPS.index((b, j0, width))
+                    piece = min(width, PIECE[g])
                     for n, c0 in enumerate(range(j0, j0 + width, piece)):
-                        after(step + 1 + n, lambda b=b, c0=c0, piece=piece: contrast(b, c0, piece))
-                        after(step + 2 + n, lambda b=b, c0=c0, piece=piece: quantise_h(b, c0, piece))
+                        after(step + n + 0, lambda g=g, b=b, c0=c0, piece=piece: contrast(g, b, c0, piece))
+                        after(step + n + 1 + 0, lambda b=b, c0=c0, piece=piece: quantise_h(b, c0, piece))
                     if b == 1:
-                        after(step + 1 + width // piece, lambda j0=j0, width=width: features(j0, width))
+                        after(step + 0 + width // piece, lambda j0=j0, width=width: features(j0, width))
             if 0 <= step - 1 < len(units):
                 inverse_root(step - 1)
             for work in later.get(step, []):

@@ -1,7 +1,6 @@
 from contextlib import ExitStack
 
 import concourse.mybir as mybir
-from concourse.masks import make_identity
 
 K, K2, T, S, H, N = 1024, 512, 4096, 1024, 1024, 512
 FLOPS = 2 * (K * H * S + K2 * H * S + H * N * S)
@@ -23,13 +22,10 @@ PACK = 4
 PASS = P * PACK
 BANK = 512
 HALF = 512
+QUADRANTS = 4
 GROUPS = [(0, 0, 512), (0, 512, 512), (1, 0, 512), (1, 512, 256), (1, 768, 128), (1, 896, 128)]
-H1V = [(0, 0, 0), (0, 0, 1), (0, 0, 2), (0, 0, 3), (0, 1, 0), (0, 1, 1), (0, 1, 2), (0, 1, 3)]
-CAST = "vvvvvv"
-MODE = "ppppppppppppppss"
-M6 = "ppppvv"
-OUTE = "ssssssss"
-PIECE = [256,256,256,256,128,128]
+PIECE = 256
+GAIN_B_ON_VECTOR = 6
 
 
 def tile_list_sail_trim_contrast_kernel(tc, tab_words, tab_scales, offs, xs_words, xs_scales, w1, w2_words, w2_scales, gain, w3, out):
@@ -40,9 +36,8 @@ def tile_list_sail_trim_contrast_kernel(tc, tab_words, tab_scales, offs, xs_word
         casts = ctx.enter_context(tc.tile_pool(name="casts", bufs=2))
         ring = ctx.enter_context(tc.tile_pool(name="ring", bufs=4))
         hring = ctx.enter_context(tc.tile_pool(name="hring", bufs=3))
-        psum_ab = ctx.enter_context(tc.psum_pool(name="psum_ab", bufs=4))
-        psum_x = ctx.enter_context(tc.psum_pool(name="psum_x", bufs=2))
-        psum_o = ctx.enter_context(tc.psum_pool(name="psum_o", bufs=2))
+        psum_a = ctx.enter_context(tc.psum_pool(name="psum_a", bufs=4))
+        psum_o = ctx.enter_context(tc.psum_pool(name="psum_o", bufs=4))
 
         offsets = keep.tile([P, S // 16], U16, name="offsets")
         tabw = [keep.tile([P, T], I32, name=f"tabw{a}", align_bytes=64) for a in range(2)]
@@ -51,25 +46,23 @@ def tile_list_sail_trim_contrast_kernel(tc, tab_words, tab_scales, offs, xs_word
         xss = keep.tile([P, S], U8, name="xss", align_bytes=64)
         w2w = keep.tile([P, 2 * H], U8, name="w2w", align_bytes=64)
         w2s = keep.tile([P, H], U8, name="w2s", align_bytes=64)
-        w2w_dealt = [keep.tile([P, 2 * PASS], U8, name=f"w2wd{b}", align_bytes=64) for b in range(2)]
-        w2s_dealt = [keep.tile([P, PASS], U8, name=f"w2sd{b}", align_bytes=64) for b in range(2)]
+        w2w_dealt = [keep.tile([P, 2 * PASS], U8, name=f"w2wd{g}", align_bytes=64) for g in range(2)]
+        w2s_dealt = [keep.tile([P, PASS], U8, name=f"w2sd{g}", align_bytes=64) for g in range(2)]
         gains = keep.tile([P, 2, PACK], F32, name="gains")
         warm = keep.tile([P, 8], F32, name="warm")
         vw = [[keep.tile([P, HALF], U32, name=f"vw{a}{jh}", align_bytes=64) for jh in range(2)] for a in range(2)]
         vs = [keep.tile([P, HALF], U8, name=f"vs{jh}", align_bytes=64) for jh in range(2)]
-        w1w = [[keep.tile([P, PASS], U32, name=f"w1w{a}{b}", align_bytes=64) for b in range(2)] for a in range(2)]
-        w1s = [[keep.tile([P, PASS], U8, name=f"w1s{a}{b}", align_bytes=64) for b in range(2)] for a in range(2)]
-        w3w = [keep.tile([P, N], U32, name=f"w3w{b}", align_bytes=64) for b in range(2)]
-        w3s = [keep.tile([P, N], U8, name=f"w3s{b}", align_bytes=64) for b in range(2)]
-        hw = [[keep.tile([P, HALF], U32, name=f"hw{b}{jh}", align_bytes=64) for jh in range(2)] for b in range(2)]
-        hs = [[keep.tile([P, HALF], U8, name=f"hs{b}{jh}", align_bytes=64) for jh in range(2)] for b in range(2)]
-        num = [[keep.tile([P, PACK, HALF], F32, name=f"num{b}{jh}", align_bytes=64) for jh in range(2)] for b in range(2)]
-        den = [[keep.tile([P, PACK, HALF], F32, name=f"den{b}{jh}", align_bytes=64) for jh in range(2)] for b in range(2)]
+        w1w = [[keep.tile([P, PASS], U32, name=f"w1w{a}{g}", align_bytes=64) for g in range(2)] for a in range(2)]
+        w1s = [[keep.tile([P, PASS], U8, name=f"w1s{a}{g}", align_bytes=64) for g in range(2)] for a in range(2)]
+        w3w = [keep.tile([P, N], U32, name=f"w3w{g}", align_bytes=64) for g in range(2)]
+        w3s = [keep.tile([P, N], U8, name=f"w3s{g}", align_bytes=64) for g in range(2)]
+        hw = [[keep.tile([P, HALF], U32, name=f"hw{g}{jh}", align_bytes=64) for jh in range(2)] for g in range(2)]
+        hs = [[keep.tile([P, HALF], U8, name=f"hs{g}{jh}", align_bytes=64) for jh in range(2)] for g in range(2)]
+        num = [[keep.tile([P, PACK, HALF], F32, name=f"num{g}{jh}", align_bytes=64) for jh in range(2)] for g in range(2)]
+        den = [[keep.tile([P, PACK, HALF], F32, name=f"den{g}{jh}", align_bytes=64) for jh in range(2)] for g in range(2)]
 
         nc.gpsimd.memset(w2s[:].bitcast(I32), 0)
         nc.gpsimd.memset(xss[:].bitcast(I32), 0)
-        identity = keep.tile([P, P], F32, name="identity")
-        make_identity(nc, identity[:])
         nc.vector.memset(warm[:], 1.0)
         nc.vector.memset(tabs[:].bitcast(I32), 0)
         nc.scalar.activation(warm[:], warm[:], ACT.Abs_reciprocal_sqrt, bias=1.0)
@@ -77,95 +70,88 @@ def tile_list_sail_trim_contrast_kernel(tc, tab_words, tab_scales, offs, xs_word
         w1_raw = {}
         w3_raw = {}
 
-        def load_w1(a, b):
-            w1_raw[a, b] = raws.tile([P, PACK, PASS], F32, name="raw")
-            rows = w1[PASS * a : PASS * (a + 1), PASS * b : PASS * (b + 1)]
-            nc.sync.dma_start(w1_raw[a, b][:], rows.rearrange("(p i) c -> p i c", i=PACK))
+        def load_w1(a, g):
+            w1_raw[a, g] = raws.tile([P, PACK, PASS], F32, name="raw")
+            rows = w1[PASS * a : PASS * (a + 1), PASS * g : PASS * (g + 1)]
+            nc.sync.dma_start(w1_raw[a, g][:], rows.rearrange("(p i) c -> p i c", i=PACK))
 
-        def load_w3(b):
-            w3_raw[b] = raws.tile([P, PACK, N], F32, name="raw")
-            nc.sync.dma_start(w3_raw[b][:], w3[PASS * b : PASS * (b + 1), :].rearrange("(p i) c -> p i c", i=PACK))
+        def load_w3(g):
+            w3_raw[g] = raws.tile([P, PACK, N], F32, name="raw")
+            nc.sync.dma_start(w3_raw[g][:], w3[PASS * g : PASS * (g + 1), :].rearrange("(p i) c -> p i c", i=PACK))
+
+        def load_scale_rows(scales, rows, first):
+            for q in range(QUADRANTS):
+                nc.sync.dma_start(scales[32 * q + first : 32 * q + first + 4, :].bitcast(I32), rows[4 * q : 4 * q + 4, :].bitcast(I32))
 
         nc.sync.dma_start(w2w[:].bitcast(I32), w2_words[0].bitcast(I32))
+        load_scale_rows(w2s, w2_scales[0], 0)
         nc.sync.dma_start(xsw[:], xs_words[0].rearrange("p c i -> p (c i)").bitcast(I32))
-        nc.sync.dma_start(offsets[:], offs)
-        for q in range(4):
-            nc.sync.dma_start(w2s[32 * q : 32 * q + 4, :].bitcast(I32), w2_scales[0, 4 * q : 4 * q + 4, :].bitcast(I32))
+        load_scale_rows(xss, xs_scales[0], 0)
+        nc.sync.dma_start(gains[:], gain.rearrange("(g p t) -> p g t", g=2, t=PACK))
         load_w1(0, 0)
-        for q in range(4):
-            nc.sync.dma_start(xss[32 * q : 32 * q + 4, :].bitcast(I32), xs_scales[0, 4 * q : 4 * q + 4, :].bitcast(I32))
-        nc.sync.dma_start(gains[:], gain.rearrange("(b p t) -> p b t", b=2, t=PACK))
+        nc.sync.dma_start(offsets[:], offs)
+        load_scale_rows(tabs, tab_scales[0], 0)
         load_w1(1, 0)
-        for q in range(4):
-            nc.sync.dma_start(tabs[32 * q : 32 * q + 8, :].bitcast(I32), tab_scales[:, 4 * q : 4 * q + 4, :].bitcast(I32))
-        nc.sync.dma_start(tabw[0][:], tab_words[0].rearrange("p t i -> p (t i)").bitcast(I32))
-        nc.sync.dma_start(tabw[1][:], tab_words[1].rearrange("p t i -> p (t i)").bitcast(I32))
+        load_scale_rows(tabs, tab_scales[1], 4)
+        for a in range(2):
+            nc.sync.dma_start(tabw[a][:], tab_words[a].rearrange("p t i -> p (t i)").bitcast(I32))
         load_w1(0, 1)
         load_w1(1, 1)
         load_w3(0)
         load_w3(1)
 
-        def deal_w2(b):
+        def deal_w2(g):
             nc.vector.tensor_copy(
-                w2w_dealt[b][:].bitcast(U16).rearrange("p (t m) -> p t m", t=PACK),
-                w2w[:, 2 * PASS * b : 2 * PASS * (b + 1)].bitcast(U16).rearrange("p (m t) -> p t m", t=PACK),
+                w2w_dealt[g][:].bitcast(U16).rearrange("p (t m) -> p t m", t=PACK),
+                w2w[:, 2 * PASS * g : 2 * PASS * (g + 1)].bitcast(U16).rearrange("p (m t) -> p t m", t=PACK),
             )
             nc.vector.tensor_copy(
-                w2s_dealt[b][:].rearrange("p (t m) -> p t m", t=PACK),
-                w2s[:, PASS * b : PASS * (b + 1)].rearrange("p (m t) -> p t m", t=PACK),
+                w2s_dealt[g][:].rearrange("p (t m) -> p t m", t=PACK),
+                w2s[:, PASS * g : PASS * (g + 1)].rearrange("p (m t) -> p t m", t=PACK),
             )
 
-        def sensors(b, jh, ts=range(PACK)):
+        def sensors(g, jh):
             cols = slice(HALF * jh, HALF * (jh + 1))
-            for t in ts:
-                pool, tag = [(psum_o, "bank_o"), (psum_x, "bank_x"), (psum_ab, "bank_ab"), (psum_o, "bank_o")][t]
+            for t in range(PACK):
+                pool, tag = (psum_o, "bank_o") if t % 2 == 0 else (psum_a, "bank_a")
                 bank = pool.tile([P, BANK], F32, name=tag)
                 nc.tensor.matmul_mx(
                     out=bank[:],
-                    lhsT=w2w_dealt[b][:, 2 * P * t : 2 * P * (t + 1)].bitcast(FP4X4),
-                    lhsT_scale=w2s_dealt[b][:, P * t : P * (t + 1)],
+                    lhsT=w2w_dealt[g][:, 2 * P * t : 2 * P * (t + 1)].bitcast(FP4X4),
+                    lhsT_scale=w2s_dealt[g][:, P * t : P * (t + 1)],
                     rhs=xsw[:, cols].bitcast(FP8X4),
                     rhs_scale=xss[:, cols],
                     start=True,
                     stop=True,
                 )
-                nc.scalar.activation(den[b][jh][:, t, :], bank[:], ACT.Abs, scale=0.5)
-                if (b, jh, t) in H1V:
-                    nc.vector.tensor_scalar_mul(num[b][jh][:, t, :], bank[:], gains[:, b, t : t + 1])
+                nc.scalar.activation(den[g][jh][:, t, :], bank[:], ACT.Abs)
+                if PACK * (2 * g + jh) + t < GAIN_B_ON_VECTOR:
+                    nc.vector.tensor_scalar_mul(num[g][jh][:, t, :], bank[:], gains[:, g, t : t + 1])
                 else:
-                    nc.scalar.activation(num[b][jh][:, t, :], bank[:], ACT.Copy, scale=gains[:, b, t : t + 1])
+                    nc.scalar.activation(num[g][jh][:, t, :], bank[:], ACT.Copy, scale=gains[:, g, t : t + 1])
 
         rounded = {}
 
-        def caster(which):
-            if which == "g":
-                return lambda dst, src: nc.gpsimd.tensor_scalar(dst, src, 1.0, 0.0, ALU.mult, ALU.add)
-            return nc.vector.tensor_copy if which == "v" else nc.scalar.copy
-
-        def round_w1(a, b, part=0, parts=1):
-            if part == 0:
-                pool, tag = (casts, "rounded") if b == 0 else (keep, "tabw1")
-                rounded["w1", a, b] = pool.tile([P, PASS * PACK], BF16, name=tag, align_bytes=64)
-            ms = slice(P // parts * part, P // parts * (part + 1))
-            caster(CAST[2 * b + a])(
-                rounded["w1", a, b][:].rearrange("p (t m i) -> p m i t", t=PACK, i=PACK)[:, ms],
-                w1_raw[a, b][:].rearrange("p i (m t) -> p m i t", t=PACK)[:, ms],
+        def round_w1(a, g):
+            pool, tag = (casts, "rounded") if g == 0 else (keep, "tabw1")
+            rounded["w1", a, g] = pool.tile([P, PASS * PACK], BF16, name=tag, align_bytes=64)
+            nc.vector.tensor_copy(
+                rounded["w1", a, g][:].rearrange("p (t m i) -> p m i t", t=PACK, i=PACK),
+                w1_raw[a, g][:].rearrange("p i (m t) -> p m i t", t=PACK),
             )
 
-        def quantise_w1(a, b):
-            nc.vector.quantize_mx(out=w1w[a][b][:].bitcast(FP8X4), scales=w1s[a][b][:], in_=rounded["w1", a, b][:])
+        def quantise_w1(a, g):
+            nc.vector.quantize_mx(out=w1w[a][g][:].bitcast(FP8X4), scales=w1s[a][g][:], in_=rounded["w1", a, g][:])
 
-        def round_w3(b, part=0, parts=1):
-            if part == 0:
-                rounded["w3", b] = keep.tile([P, N * PACK], BF16, name="tabw1", align_bytes=64)
-            cs = slice(P // parts * part, P // parts * (part + 1))
-            caster(CAST[4 + b])(
-                rounded["w3", b][:].rearrange("p (c e i) -> p c i e", e=4, i=PACK)[:, cs],
-                w3_raw[b][:].rearrange("p i (c e) -> p c i e", e=4)[:, cs],
+        def round_w3(g):
+            rounded["w3", g] = keep.tile([P, N * PACK], BF16, name="tabw1", align_bytes=64)
+            nc.scalar.copy(
+                rounded["w3", g][:].rearrange("p (c e i) -> p c i e", e=4, i=PACK),
+                w3_raw[g][:].rearrange("p i (c e) -> p c i e", e=4),
             )
 
-        def quantise_w3(b):
-            nc.vector.quantize_mx(out=w3w[b][:].bitcast(FP8X4), scales=w3s[b][:], in_=rounded["w3", b][:])
+        def quantise_w3(g):
+            nc.vector.quantize_mx(out=w3w[g][:].bitcast(FP8X4), scales=w3s[g][:], in_=rounded["w3", g][:])
 
         def part_of_list(jh):
             return offsets[:, HALF // 16 * jh : HALF // 16 * (jh + 1)]
@@ -177,128 +163,110 @@ def tile_list_sail_trim_contrast_kernel(tc, tab_words, tab_scales, offs, xs_word
             nc.vector.tensor_copy(vs[jh][:], tabs[:].indirect(part_of_list(jh)))
 
         units = []
-        for b, j0, width in GROUPS:
+        for g, j0, width in GROUPS:
             nt = BANK // width
             for t0 in range(0, PACK, nt):
-                units.append((b, j0, width, t0, nt))
+                units.append((g, j0, width, t0, nt))
         banks = {}
+        mags = {}
 
         def view(tiles, u):
-            b, j0, width, t0, nt = units[u]
-            return tiles[b][j0 // HALF][:, t0 : t0 + nt, j0 % HALF : j0 % HALF + width]
+            g, j0, width, t0, nt = units[u]
+            return tiles[g][j0 // HALF][:, t0 : t0 + nt, j0 % HALF : j0 % HALF + width]
 
         def shapes(u):
-            b, j0, width, t0, nt = units[u]
+            g, j0, width, t0, nt = units[u]
             jh = j0 // HALF
             cols = slice(j0 % HALF, j0 % HALF + width)
-            banks[u] = psum_ab.tile([P, nt, width], F32, name="bank_ab")
+            banks[u] = psum_a.tile([P, nt, width], F32, name="bank_a")
             for t in range(t0, t0 + nt):
                 for a in range(2):
                     nc.tensor.matmul_mx(
                         out=banks[u][:, t - t0, :],
-                        lhsT=w1w[a][b][:, P * t : P * (t + 1)].bitcast(FP8X4),
-                        lhsT_scale=w1s[a][b][:, P * t : P * (t + 1)],
+                        lhsT=w1w[a][g][:, P * t : P * (t + 1)].bitcast(FP8X4),
+                        lhsT_scale=w1s[a][g][:, P * t : P * (t + 1)],
                         rhs=vw[a][jh][:, cols].bitcast(FP8X4),
                         rhs_scale=vs[jh][4 * a :, cols],
                         start=(a == 0),
                         stop=(a == 1),
                     )
 
-        mags = {}
-        sums = {}
-
-        def positive_part(u):
-            if MODE[u] == "v":
-                nc.vector.scalar_tensor_tensor(view(den, u), banks[u][:], 0.0, view(den, u), ALU.max, ALU.add)
-            else:
-                b, j0, width, t0, nt = units[u]
-                mags[u] = ring.tile([P, nt, width], F32, name="mag")
-                nc.scalar.activation(mags[u][:], banks[u][:], ACT.Abs, scale=0.5)
+        def magnitude(u):
+            g, j0, width, t0, nt = units[u]
+            mags[u] = ring.tile([P, nt, width], F32, name="mag")
+            nc.scalar.activation(mags[u][:], banks[u][:], ACT.Abs)
 
         def numerator(u):
-            b, j0, width, t0, nt = units[u]
+            g, j0, width, t0, nt = units[u]
             for t in range(nt):
                 part = view(num, u)[:, t, :]
-                nc.vector.scalar_tensor_tensor(part, banks[u][:, t, :], gains[:, b, t0 + t : t0 + t + 1], part, ALU.mult, ALU.subtract)
+                nc.vector.scalar_tensor_tensor(part, banks[u][:, t, :], gains[:, g, t0 + t : t0 + t + 1], part, ALU.mult, ALU.subtract)
 
         def both_sizes(u):
-            if MODE[u] == "v":
-                nc.vector.scalar_tensor_tensor(view(den, u), banks[u][:], -0.5, view(den, u), ALU.mult, ALU.add)
-            elif MODE[u] == "p":
-                b, j0, width, t0, nt = units[u]
-                sums[u] = psum_x.tile([P, nt, width], F32, name="bank_x")
-                for t in range(nt):
-                    for c0 in range(0, width, P):
-                        block = slice(c0, c0 + P)
-                        nc.tensor.matmul(sums[u][:, t, block], view(den, u)[:, t, block], identity[:], start=True, stop=False, is_transpose=True)
-                        nc.tensor.matmul(sums[u][:, t, block], mags[u][:, t, block], identity[:], start=False, stop=True, is_transpose=True)
-            else:
-                engine = nc.vector if MODE[u] == "s" else nc.gpsimd
-                engine.tensor_tensor(view(den, u), mags[u][:], view(den, u), ALU.add)
+            nc.vector.tensor_tensor(view(den, u), mags[u][:], view(den, u), ALU.add)
 
         def inverse_root(u):
-            size = sums[u][:] if MODE[u] == "p" else view(den, u)
-            nc.scalar.activation(view(den, u), size, ACT.Abs_reciprocal_sqrt, bias=1.0, scale=2.0)
+            nc.scalar.activation(view(den, u), view(den, u), ACT.Abs_reciprocal_sqrt, bias=1.0)
 
         def inverse(u):
             nc.scalar.activation(view(den, u), view(den, u), ACT.Square)
 
         h_rounded = {}
 
-        def contrast(g, b, j0, width):
-            jh = j0 // HALF
-            h_rounded[b, j0] = hring.tile([P, width, PACK], BF16, name="h_rounded", align_bytes=64)
-            step = P if M6[g] == "p" else width
-            for c0 in range(0, width, step):
-                cols = slice(j0 % HALF + c0, j0 % HALF + c0 + step)
-                if M6[g] == "p":
-                    back = psum_o.tile([P, PACK, P], F32, name="bank_o")
-                    for t in range(PACK):
-                        nc.tensor.transpose(back[:, t, :], den[b][jh][:, t, cols], identity[:])
-                    inverses = back[:]
-                else:
-                    inverses = den[b][jh][:, :, cols]
-                nc.vector.tensor_tensor(
-                    h_rounded[b, j0][:, c0 : c0 + step, :].rearrange("p (c e) t -> p c t e", e=2),
-                    inverses.rearrange("p t (c e) -> p c t e", e=2),
-                    num[b][jh][:, :, cols].rearrange("p t (c e) -> p c t e", e=2),
-                    ALU.mult,
-                )
-
-        def quantise_h(b, j0, width):
+        def contrast(g, j0, width):
             jh = j0 // HALF
             cols = slice(j0 % HALF, j0 % HALF + width)
-            nc.vector.quantize_mx(out=hw[b][jh][:, cols].bitcast(FP8X4), scales=hs[b][jh][:, cols], in_=h_rounded[b, j0][:].rearrange("p c t -> p (c t)"))
+            h_rounded[g, j0] = hring.tile([P, width, PACK], BF16, name="h_rounded", align_bytes=64)
+            nc.vector.tensor_tensor(
+                h_rounded[g, j0][:].rearrange("p (c e) t -> p c t e", e=2),
+                den[g][jh][:, :, cols].rearrange("p t (c e) -> p c t e", e=2),
+                num[g][jh][:, :, cols].rearrange("p t (c e) -> p c t e", e=2),
+                ALU.mult,
+            )
+
+        def quantise_h(g, j0, width):
+            jh = j0 // HALF
+            cols = slice(j0 % HALF, j0 % HALF + width)
+            nc.vector.quantize_mx(out=hw[g][jh][:, cols].bitcast(FP8X4), scales=hs[g][jh][:, cols], in_=h_rounded[g, j0][:].rearrange("p c t -> p (c t)"))
 
         out_rows = out.rearrange("(n p) j -> p n j", p=P)
 
-        stored = []
-
-        def features(j0, width):
+        def feature_pass(bank, n, g, j0, width):
             jh = j0 // HALF
             cols = slice(j0 % HALF, j0 % HALF + width)
+            nc.tensor.matmul_mx(
+                out=bank,
+                lhsT=w3w[g][:, P * n : P * (n + 1)].bitcast(FP8X4),
+                lhsT_scale=w3s[g][:, P * n : P * (n + 1)],
+                rhs=hw[g][jh][:, cols].bitcast(FP8X4),
+                rhs_scale=hs[g][jh][:, cols],
+                start=(g == 0),
+                stop=(g == 1),
+            )
+
+        def features(j0, width):
             nn = BANK // width
             for n0 in range(0, N // P, nn):
-                pool, tag = {"a": (psum_ab, "bank_ab"), "x": (psum_x, "bank_x"), "o": (psum_o, "bank_o")}["aaaaaaaa"[len(stored)]]
-                bank = pool.tile([P, nn, width], F32, name=tag)
+                bank = psum_o.tile([P, nn, width], F32, name="bank_o")
                 for n in range(n0, n0 + nn):
-                    for b in range(2):
-                        nc.tensor.matmul_mx(
-                            out=bank[:, n - n0, :],
-                            lhsT=w3w[b][:, P * n : P * (n + 1)].bitcast(FP8X4),
-                            lhsT_scale=w3s[b][:, P * n : P * (n + 1)],
-                            rhs=hw[b][jh][:, cols].bitcast(FP8X4),
-                            rhs_scale=hs[b][jh][:, cols],
-                            start=(b == 0),
-                            stop=(b == 1),
-                        )
+                    for g in range(2):
+                        feature_pass(bank[:, n - n0, :], n, g, j0, width)
                 staged = ring.tile([P, nn, width], F32, name="staged")
-                stored.append(n0)
-                if OUTE[len(stored) - 1] == "s":
-                    nc.scalar.copy(staged[:], bank[:])
-                else:
-                    nc.vector.tensor_copy(staged[:], bank[:])
+                nc.scalar.copy(staged[:], bank[:])
                 nc.sync.dma_start(out_rows[:, n0 : n0 + nn, j0 : j0 + width], staged[:])
+
+        def last_features(j0, width):
+            staged = ring.tile([P, N // P, width], F32, name="staged")
+            sums = [psum_a.tile([P, width], F32, name="bank_a") for n in range(N // P)]
+            for g in range(2):
+                for n in range(N // P):
+                    feature_pass(sums[n][:], n, g, j0, width)
+            for n in range(N // P):
+                if n % 2 == 0:
+                    nc.vector.tensor_copy(staged[:, n, :], sums[n][:])
+                else:
+                    nc.scalar.copy(staged[:, n, :], sums[n][:])
+            nc.sync.dma_start(out_rows[:, :, j0 : j0 + width], staged[:])
 
         deal_w2(0)
         sensors(0, 0)
@@ -316,42 +284,45 @@ def tile_list_sail_trim_contrast_kernel(tc, tab_words, tab_scales, offs, xs_word
         sensors(1, 0)
         sensors(1, 1)
 
-        later = {
-            0: [lambda: gather_words(1, 1)],
-            2: [lambda: round_w1(0, 1)],
-            3: [lambda: quantise_w1(0, 1)],
-            4: [lambda: round_w1(1, 1)],
-            5: [lambda: quantise_w1(1, 1)],
-            6: [lambda: round_w3(0)],
-            7: [lambda: quantise_w3(0)],
-            8: [lambda: round_w3(1)],
-            9: [lambda: quantise_w3(1)],
-        }
+        later = {0: [lambda: gather_words(1, 1)]}
 
         def after(step, work):
             later.setdefault(step, []).append(work)
 
+        weights_left = [
+            lambda: round_w1(0, 1),
+            lambda: quantise_w1(0, 1),
+            lambda: round_w1(1, 1),
+            lambda: quantise_w1(1, 1),
+            lambda: round_w3(0),
+            lambda: quantise_w3(0),
+            lambda: round_w3(1),
+            lambda: quantise_w3(1),
+        ]
+        for n, work in enumerate(weights_left):
+            after(2 + n, work)
+
         shapes(0)
         shapes(1)
-        for step in range(len(units) + 10):
+        for step in range(len(units) + 4):
             if step + 2 < len(units):
                 shapes(step + 2)
             if step < len(units):
-                positive_part(step)
+                magnitude(step)
             if 0 <= step - 1 < len(units):
                 numerator(step - 1)
                 both_sizes(step - 1)
             if 0 <= step - 2 < len(units):
                 inverse(step - 2)
-                b, j0, width, t0, nt = units[step - 2]
+                g, j0, width, t0, nt = units[step - 2]
                 if t0 + nt == PACK:
-                    g = GROUPS.index((b, j0, width))
-                    piece = min(width, PIECE[g])
+                    piece = min(width, PIECE)
                     for n, c0 in enumerate(range(j0, j0 + width, piece)):
-                        after(step + n + 0, lambda g=g, b=b, c0=c0, piece=piece: contrast(g, b, c0, piece))
-                        after(step + n + 1 + 0, lambda b=b, c0=c0, piece=piece: quantise_h(b, c0, piece))
-                    if b == 1:
-                        after(step + 0 + width // piece, lambda j0=j0, width=width: features(j0, width))
+                        after(step + n, lambda g=g, c0=c0, piece=piece: contrast(g, c0, piece))
+                        after(step + n + 1, lambda g=g, c0=c0, piece=piece: quantise_h(g, c0, piece))
+                    if g == 1:
+                        product = last_features if j0 + width == S else features
+                        after(step + width // piece, lambda product=product, j0=j0, width=width: product(j0, width))
             if 0 <= step - 1 < len(units):
                 inverse_root(step - 1)
             for work in later.get(step, []):

@@ -25,7 +25,7 @@ HALF = 512
 QUADRANTS = 4
 GROUPS = [(0, 0, 512), (0, 512, 512), (1, 0, 512), (1, 512, 256), (1, 768, 128), (1, 896, 128)]
 PIECE = 256
-GAIN_B_ON_VECTOR = 6
+GAIN_B_ON_VECTOR = 7
 
 
 def tile_list_sail_trim_contrast_kernel(tc, tab_words, tab_scales, offs, xs_words, xs_scales, w1, w2_words, w2_scales, gain, w3, out):
@@ -51,7 +51,8 @@ def tile_list_sail_trim_contrast_kernel(tc, tab_words, tab_scales, offs, xs_word
         gains = keep.tile([P, 2, PACK], F32, name="gains")
         warm = keep.tile([P, 8], F32, name="warm")
         vw = [[keep.tile([P, HALF], U32, name=f"vw{a}{jh}", align_bytes=64) for jh in range(2)] for a in range(2)]
-        vs = [keep.tile([P, HALF], U8, name=f"vs{jh}", align_bytes=64) for jh in range(2)]
+        picked = keep.tile([P, S], U8, name="picked", align_bytes=64)
+        vs = [keep.tile([P, S], U8, name=f"vs{a}", align_bytes=64) for a in range(2)]
         w1w = [[keep.tile([P, PASS], U32, name=f"w1w{a}{g}", align_bytes=64) for g in range(2)] for a in range(2)]
         w1s = [[keep.tile([P, PASS], U8, name=f"w1s{a}{g}", align_bytes=64) for g in range(2)] for a in range(2)]
         w3w = [keep.tile([P, N], U32, name=f"w3w{g}", align_bytes=64) for g in range(2)]
@@ -63,6 +64,8 @@ def tile_list_sail_trim_contrast_kernel(tc, tab_words, tab_scales, offs, xs_word
 
         nc.gpsimd.memset(w2s[:].bitcast(I32), 0)
         nc.gpsimd.memset(xss[:].bitcast(I32), 0)
+        for a in range(2):
+            nc.gpsimd.memset(vs[a][:].bitcast(I32), 0)
         nc.vector.memset(warm[:], 1.0)
         nc.vector.memset(tabs[:].bitcast(I32), 0)
         nc.scalar.activation(warm[:], warm[:], ACT.Abs_reciprocal_sqrt, bias=1.0)
@@ -79,22 +82,24 @@ def tile_list_sail_trim_contrast_kernel(tc, tab_words, tab_scales, offs, xs_word
             w3_raw[g] = raws.tile([P, PACK, N], F32, name="raw")
             nc.sync.dma_start(w3_raw[g][:], w3[PASS * g : PASS * (g + 1), :].rearrange("(p i) c -> p i c", i=PACK))
 
-        def load_scale_rows(scales, rows, first):
-            for q in range(QUADRANTS):
-                nc.sync.dma_start(scales[32 * q + first : 32 * q + first + 4, :].bitcast(I32), rows[4 * q : 4 * q + 4, :].bitcast(I32))
+        def load_scale_rows(scales, rows):
+            for r in range(4):
+                nc.sync.dma_start(scales[r:P:32, :].bitcast(I32), rows[r:16:4, :].bitcast(I32))
 
         nc.sync.dma_start(w2w[:].bitcast(I32), w2_words[0].bitcast(I32))
-        load_scale_rows(w2s, w2_scales[0], 0)
+        load_scale_rows(w2s, w2_scales[0])
         nc.sync.dma_start(xsw[:], xs_words[0].rearrange("p c i -> p (c i)").bitcast(I32))
-        load_scale_rows(xss, xs_scales[0], 0)
-        nc.sync.dma_start(gains[:], gain.rearrange("(g p t) -> p g t", g=2, t=PACK))
-        load_w1(0, 0)
+        load_scale_rows(xss, xs_scales[0])
         nc.sync.dma_start(offsets[:], offs)
-        load_scale_rows(tabs, tab_scales[0], 0)
+        nc.sync.dma_start(tabs[0:P:4, :].bitcast(I32), tab_scales.rearrange("a q t -> (a q) t").bitcast(I32))
+        load_w1(0, 0)
+        nc.sync.dma_start(gains[:], gain.rearrange("(g p t) -> p g t", g=2, t=PACK))
         load_w1(1, 0)
-        load_scale_rows(tabs, tab_scales[1], 4)
+        nc.vector.tensor_copy(picked[:], tabs[:].indirect(offsets[:]))
         for a in range(2):
             nc.sync.dma_start(tabw[a][:], tab_words[a].rearrange("p t i -> p (t i)").bitcast(I32))
+            for r in range(4):
+                nc.sync.dma_start(vs[a][r:P:32, :].bitcast(I32), picked[64 * a + 4 * r : 64 * (a + 1) : 16, :].bitcast(I32))
         load_w1(0, 1)
         load_w1(1, 1)
         load_w3(0)
@@ -113,7 +118,7 @@ def tile_list_sail_trim_contrast_kernel(tc, tab_words, tab_scales, offs, xs_word
         def sensors(g, jh):
             cols = slice(HALF * jh, HALF * (jh + 1))
             for t in range(PACK):
-                pool, tag = (psum_o, "bank_o") if t % 2 == 0 else (psum_a, "bank_a")
+                pool, tag = (psum_o, "bank_o") if t % 2 == 0 or g == 1 else (psum_a, "bank_a")
                 bank = pool.tile([P, BANK], F32, name=tag)
                 nc.tensor.matmul_mx(
                     out=bank[:],
@@ -159,9 +164,6 @@ def tile_list_sail_trim_contrast_kernel(tc, tab_words, tab_scales, offs, xs_word
         def gather_words(a, jh):
             nc.vector.tensor_copy(vw[a][jh][:], tabw[a][:].bitcast(U32).indirect(part_of_list(jh)))
 
-        def gather_scales(jh):
-            nc.vector.tensor_copy(vs[jh][:], tabs[:].indirect(part_of_list(jh)))
-
         units = []
         for g, j0, width in GROUPS:
             nt = BANK // width
@@ -186,7 +188,7 @@ def tile_list_sail_trim_contrast_kernel(tc, tab_words, tab_scales, offs, xs_word
                         lhsT=w1w[a][g][:, P * t : P * (t + 1)].bitcast(FP8X4),
                         lhsT_scale=w1s[a][g][:, P * t : P * (t + 1)],
                         rhs=vw[a][jh][:, cols].bitcast(FP8X4),
-                        rhs_scale=vs[jh][4 * a :, cols],
+                        rhs_scale=vs[a][:, j0 : j0 + width],
                         start=(a == 0),
                         stop=(a == 1),
                     )
@@ -275,11 +277,9 @@ def tile_list_sail_trim_contrast_kernel(tc, tab_words, tab_scales, offs, xs_word
         round_w1(1, 0)
         quantise_w1(0, 0)
         quantise_w1(1, 0)
-        gather_scales(0)
         gather_words(0, 0)
         gather_words(1, 0)
         sensors(0, 1)
-        gather_scales(1)
         gather_words(0, 1)
         sensors(1, 0)
         sensors(1, 1)

from contextlib import ExitStack

import concourse.mybir as mybir

K, K2, T, S, H, N = 1024, 512, 4096, 1024, 1024, 512
FLOPS = 2 * (K * H * S + K2 * H * S + H * N * S)
BYTES = (K * T + K // 32 * T) + 2 * 128 * 64 + (K2 * S + K2 // 32 * S) + 4 * K * H + (K2 * H // 2 + K2 // 32 * H) + 4 * H + 4 * H * N + 4 * N * S

F32 = mybir.dt.float32
BF16 = mybir.dt.bfloat16
I32 = mybir.dt.int32
U32 = mybir.dt.uint32
U16 = mybir.dt.uint16
U8 = mybir.dt.uint8
FP8X4 = mybir.dt.float8_e4m3fn_x4
FP4X4 = mybir.dt.float4_e2m1fn_x4
ALU = mybir.AluOpType
ACT = mybir.ActivationFunctionType

P = 128
PACK = 4
PASS = P * PACK
BANK = 512
HALF = 512
QUADRANTS = 4
GROUPS = [(0, 0, 512), (0, 512, 512), (1, 0, 512), (1, 512, 256), (1, 768, 128), (1, 896, 128)]
PIECE = 256
GAIN_B_ON_VECTOR = 7


def tile_list_sail_trim_contrast_kernel(tc, tab_words, tab_scales, offs, xs_words, xs_scales, w1, w2_words, w2_scales, gain, w3, out):
    nc = tc.nc
    with ExitStack() as ctx:
        keep = ctx.enter_context(tc.tile_pool(name="keep", bufs=1))
        raws = ctx.enter_context(tc.tile_pool(name="raws", bufs=6))
        casts = ctx.enter_context(tc.tile_pool(name="casts", bufs=2))
        ring = ctx.enter_context(tc.tile_pool(name="ring", bufs=4))
        hring = ctx.enter_context(tc.tile_pool(name="hring", bufs=3))
        psum_a = ctx.enter_context(tc.psum_pool(name="psum_a", bufs=4))
        psum_o = ctx.enter_context(tc.psum_pool(name="psum_o", bufs=4))

        offsets = keep.tile([P, S // 16], U16, name="offsets")
        tabw = [keep.tile([P, T], I32, name=f"tabw{a}", align_bytes=64) for a in range(2)]
        tabs = keep.tile([P, T], U8, name="tabs", align_bytes=64)
        xsw = keep.tile([P, S], I32, name="xsw", align_bytes=64)
        xss = keep.tile([P, S], U8, name="xss", align_bytes=64)
        w2w = keep.tile([P, 2 * H], U8, name="w2w", align_bytes=64)
        w2s = keep.tile([P, H], U8, name="w2s", align_bytes=64)
        w2w_dealt = [keep.tile([P, 2 * PASS], U8, name=f"w2wd{g}", align_bytes=64) for g in range(2)]
        w2s_dealt = [keep.tile([P, PASS], U8, name=f"w2sd{g}", align_bytes=64) for g in range(2)]
        gains = keep.tile([P, 2, PACK], F32, name="gains")
        warm = keep.tile([P, 8], F32, name="warm")
        vw = [[keep.tile([P, HALF], U32, name=f"vw{a}{jh}", align_bytes=64) for jh in range(2)] for a in range(2)]
        picked = keep.tile([P, S], U8, name="picked", align_bytes=64)
        vs = [keep.tile([P, S], U8, name=f"vs{a}", align_bytes=64) for a in range(2)]
        w1w = [[keep.tile([P, PASS], U32, name=f"w1w{a}{g}", align_bytes=64) for g in range(2)] for a in range(2)]
        w1s = [[keep.tile([P, PASS], U8, name=f"w1s{a}{g}", align_bytes=64) for g in range(2)] for a in range(2)]
        w3w = [keep.tile([P, N], U32, name=f"w3w{g}", align_bytes=64) for g in range(2)]
        w3s = [keep.tile([P, N], U8, name=f"w3s{g}", align_bytes=64) for g in range(2)]
        hw = [[keep.tile([P, HALF], U32, name=f"hw{g}{jh}", align_bytes=64) for jh in range(2)] for g in range(2)]
        hs = [[keep.tile([P, HALF], U8, name=f"hs{g}{jh}", align_bytes=64) for jh in range(2)] for g in range(2)]
        num = [[keep.tile([P, PACK, HALF], F32, name=f"num{g}{jh}", align_bytes=64) for jh in range(2)] for g in range(2)]
        den = [[keep.tile([P, PACK, HALF], F32, name=f"den{g}{jh}", align_bytes=64) for jh in range(2)] for g in range(2)]

        nc.gpsimd.memset(w2s[:].bitcast(I32), 0)
        nc.gpsimd.memset(xss[:].bitcast(I32), 0)
        for a in range(2):
            nc.gpsimd.memset(vs[a][:].bitcast(I32), 0)
        nc.vector.memset(warm[:], 1.0)
        nc.vector.memset(tabs[:].bitcast(I32), 0)
        nc.scalar.activation(warm[:], warm[:], ACT.Abs_reciprocal_sqrt, bias=1.0)

        w1_raw = {}
        w3_raw = {}

        def load_w1(a, g):
            w1_raw[a, g] = raws.tile([P, PACK, PASS], F32, name="raw")
            rows = w1[PASS * a : PASS * (a + 1), PASS * g : PASS * (g + 1)]
            nc.sync.dma_start(w1_raw[a, g][:], rows.rearrange("(p i) c -> p i c", i=PACK))

        def load_w3(g):
            w3_raw[g] = raws.tile([P, PACK, N], F32, name="raw")
            nc.sync.dma_start(w3_raw[g][:], w3[PASS * g : PASS * (g + 1), :].rearrange("(p i) c -> p i c", i=PACK))

        def load_scale_rows(scales, rows):
            for r in range(4):
                nc.sync.dma_start(scales[r:P:32, :].bitcast(I32), rows[r:16:4, :].bitcast(I32))

        nc.sync.dma_start(w2w[:].bitcast(I32), w2_words[0].bitcast(I32))
        load_scale_rows(w2s, w2_scales[0])
        nc.sync.dma_start(xsw[:], xs_words[0].rearrange("p c i -> p (c i)").bitcast(I32))
        load_scale_rows(xss, xs_scales[0])
        nc.sync.dma_start(offsets[:], offs)
        nc.sync.dma_start(tabs[0:P:4, :].bitcast(I32), tab_scales.rearrange("a q t -> (a q) t").bitcast(I32))
        load_w1(0, 0)
        nc.sync.dma_start(gains[:], gain.rearrange("(g p t) -> p g t", g=2, t=PACK))
        load_w1(1, 0)
        nc.vector.tensor_copy(picked[:], tabs[:].indirect(offsets[:]))
        for a in range(2):
            nc.sync.dma_start(tabw[a][:], tab_words[a].rearrange("p t i -> p (t i)").bitcast(I32))
            for r in range(4):
                nc.sync.dma_start(vs[a][r:P:32, :].bitcast(I32), picked[64 * a + 4 * r : 64 * (a + 1) : 16, :].bitcast(I32))
        load_w1(0, 1)
        load_w1(1, 1)
        load_w3(0)
        load_w3(1)

        def deal_w2(g):
            nc.vector.tensor_copy(
                w2w_dealt[g][:].bitcast(U16).rearrange("p (t m) -> p t m", t=PACK),
                w2w[:, 2 * PASS * g : 2 * PASS * (g + 1)].bitcast(U16).rearrange("p (m t) -> p t m", t=PACK),
            )
            nc.vector.tensor_copy(
                w2s_dealt[g][:].rearrange("p (t m) -> p t m", t=PACK),
                w2s[:, PASS * g : PASS * (g + 1)].rearrange("p (m t) -> p t m", t=PACK),
            )

        def sensors(g, jh):
            cols = slice(HALF * jh, HALF * (jh + 1))
            for t in range(PACK):
                pool, tag = (psum_o, "bank_o") if t % 2 == 0 or g == 1 else (psum_a, "bank_a")
                bank = pool.tile([P, BANK], F32, name=tag)
                nc.tensor.matmul_mx(
                    out=bank[:],
                    lhsT=w2w_dealt[g][:, 2 * P * t : 2 * P * (t + 1)].bitcast(FP4X4),
                    lhsT_scale=w2s_dealt[g][:, P * t : P * (t + 1)],
                    rhs=xsw[:, cols].bitcast(FP8X4),
                    rhs_scale=xss[:, cols],
                    start=True,
                    stop=True,
                )
                nc.scalar.activation(den[g][jh][:, t, :], bank[:], ACT.Abs)
                if PACK * (2 * g + jh) + t < GAIN_B_ON_VECTOR:
                    nc.vector.tensor_scalar_mul(num[g][jh][:, t, :], bank[:], gains[:, g, t : t + 1])
                else:
                    nc.scalar.activation(num[g][jh][:, t, :], bank[:], ACT.Copy, scale=gains[:, g, t : t + 1])

        rounded = {}

        def round_w1(a, g):
            pool, tag = (casts, "rounded") if g == 0 else (keep, "tabw1")
            rounded["w1", a, g] = pool.tile([P, PASS * PACK], BF16, name=tag, align_bytes=64)
            nc.vector.tensor_copy(
                rounded["w1", a, g][:].rearrange("p (t m i) -> p m i t", t=PACK, i=PACK),
                w1_raw[a, g][:].rearrange("p i (m t) -> p m i t", t=PACK),
            )

        def quantise_w1(a, g):
            nc.vector.quantize_mx(out=w1w[a][g][:].bitcast(FP8X4), scales=w1s[a][g][:], in_=rounded["w1", a, g][:])

        def round_w3(g):
            rounded["w3", g] = keep.tile([P, N * PACK], BF16, name="tabw1", align_bytes=64)
            nc.scalar.copy(
                rounded["w3", g][:].rearrange("p (c e i) -> p c i e", e=4, i=PACK),
                w3_raw[g][:].rearrange("p i (c e) -> p c i e", e=4),
            )

        def quantise_w3(g):
            nc.vector.quantize_mx(out=w3w[g][:].bitcast(FP8X4), scales=w3s[g][:], in_=rounded["w3", g][:])

        def part_of_list(jh):
            return offsets[:, HALF // 16 * jh : HALF // 16 * (jh + 1)]

        def gather_words(a, jh):
            nc.vector.tensor_copy(vw[a][jh][:], tabw[a][:].bitcast(U32).indirect(part_of_list(jh)))

        units = []
        for g, j0, width in GROUPS:
            nt = BANK // width
            for t0 in range(0, PACK, nt):
                units.append((g, j0, width, t0, nt))
        banks = {}
        mags = {}

        def view(tiles, u):
            g, j0, width, t0, nt = units[u]
            return tiles[g][j0 // HALF][:, t0 : t0 + nt, j0 % HALF : j0 % HALF + width]

        def shapes(u):
            g, j0, width, t0, nt = units[u]
            jh = j0 // HALF
            cols = slice(j0 % HALF, j0 % HALF + width)
            banks[u] = psum_a.tile([P, nt, width], F32, name="bank_a")
            for t in range(t0, t0 + nt):
                for a in range(2):
                    nc.tensor.matmul_mx(
                        out=banks[u][:, t - t0, :],
                        lhsT=w1w[a][g][:, P * t : P * (t + 1)].bitcast(FP8X4),
                        lhsT_scale=w1s[a][g][:, P * t : P * (t + 1)],
                        rhs=vw[a][jh][:, cols].bitcast(FP8X4),
                        rhs_scale=vs[a][:, j0 : j0 + width],
                        start=(a == 0),
                        stop=(a == 1),
                    )

        def magnitude(u):
            g, j0, width, t0, nt = units[u]
            mags[u] = ring.tile([P, nt, width], F32, name="mag")
            nc.scalar.activation(mags[u][:], banks[u][:], ACT.Abs)

        def numerator(u):
            g, j0, width, t0, nt = units[u]
            for t in range(nt):
                part = view(num, u)[:, t, :]
                nc.vector.scalar_tensor_tensor(part, banks[u][:, t, :], gains[:, g, t0 + t : t0 + t + 1], part, ALU.mult, ALU.subtract)

        def both_sizes(u):
            nc.vector.tensor_tensor(view(den, u), mags[u][:], view(den, u), ALU.add)

        def inverse_root(u):
            nc.scalar.activation(view(den, u), view(den, u), ACT.Abs_reciprocal_sqrt, bias=1.0)

        def inverse(u):
            nc.scalar.activation(view(den, u), view(den, u), ACT.Square)

        h_rounded = {}

        def contrast(g, j0, width):
            jh = j0 // HALF
            cols = slice(j0 % HALF, j0 % HALF + width)
            h_rounded[g, j0] = hring.tile([P, width, PACK], BF16, name="h_rounded", align_bytes=64)
            nc.vector.tensor_tensor(
                h_rounded[g, j0][:].rearrange("p (c e) t -> p c t e", e=2),
                den[g][jh][:, :, cols].rearrange("p t (c e) -> p c t e", e=2),
                num[g][jh][:, :, cols].rearrange("p t (c e) -> p c t e", e=2),
                ALU.mult,
            )

        def quantise_h(g, j0, width):
            jh = j0 // HALF
            cols = slice(j0 % HALF, j0 % HALF + width)
            nc.vector.quantize_mx(out=hw[g][jh][:, cols].bitcast(FP8X4), scales=hs[g][jh][:, cols], in_=h_rounded[g, j0][:].rearrange("p c t -> p (c t)"))

        out_rows = out.rearrange("(n p) j -> p n j", p=P)

        def feature_pass(bank, n, g, j0, width):
            jh = j0 // HALF
            cols = slice(j0 % HALF, j0 % HALF + width)
            nc.tensor.matmul_mx(
                out=bank,
                lhsT=w3w[g][:, P * n : P * (n + 1)].bitcast(FP8X4),
                lhsT_scale=w3s[g][:, P * n : P * (n + 1)],
                rhs=hw[g][jh][:, cols].bitcast(FP8X4),
                rhs_scale=hs[g][jh][:, cols],
                start=(g == 0),
                stop=(g == 1),
            )

        def features(j0, width):
            nn = BANK // width
            for n0 in range(0, N // P, nn):
                bank = psum_o.tile([P, nn, width], F32, name="bank_o")
                for n in range(n0, n0 + nn):
                    for g in range(2):
                        feature_pass(bank[:, n - n0, :], n, g, j0, width)
                staged = ring.tile([P, nn, width], F32, name="staged")
                nc.scalar.copy(staged[:], bank[:])
                nc.sync.dma_start(out_rows[:, n0 : n0 + nn, j0 : j0 + width], staged[:])

        def last_features(j0, width):
            staged = ring.tile([P, N // P, width], F32, name="staged")
            sums = [psum_a.tile([P, width], F32, name="bank_a") for n in range(N // P)]
            for g in range(2):
                for n in range(N // P):
                    feature_pass(sums[n][:], n, g, j0, width)
            for n in range(N // P):
                if n % 2 == 0:
                    nc.vector.tensor_copy(staged[:, n, :], sums[n][:])
                else:
                    nc.scalar.copy(staged[:, n, :], sums[n][:])
            nc.sync.dma_start(out_rows[:, :, j0 : j0 + width], staged[:])

        deal_w2(0)
        sensors(0, 0)
        deal_w2(1)
        round_w1(0, 0)
        round_w1(1, 0)
        quantise_w1(0, 0)
        quantise_w1(1, 0)
        gather_words(0, 0)
        gather_words(1, 0)
        sensors(0, 1)
        gather_words(0, 1)
        sensors(1, 0)
        sensors(1, 1)

        later = {0: [lambda: gather_words(1, 1)]}

        def after(step, work):
            later.setdefault(step, []).append(work)

        weights_left = [
            lambda: round_w1(0, 1),
            lambda: quantise_w1(0, 1),
            lambda: round_w1(1, 1),
            lambda: quantise_w1(1, 1),
            lambda: round_w3(0),
            lambda: quantise_w3(0),
            lambda: round_w3(1),
            lambda: quantise_w3(1),
        ]
        for n, work in enumerate(weights_left):
            after(2 + n, work)

        shapes(0)
        shapes(1)
        for step in range(len(units) + 4):
            if step + 2 < len(units):
                shapes(step + 2)
            if step < len(units):
                magnitude(step)
            if 0 <= step - 1 < len(units):
                numerator(step - 1)
                both_sizes(step - 1)
            if 0 <= step - 2 < len(units):
                inverse(step - 2)
                g, j0, width, t0, nt = units[step - 2]
                if t0 + nt == PACK:
                    piece = min(width, PIECE)
                    for n, c0 in enumerate(range(j0, j0 + width, piece)):
                        after(step + n, lambda g=g, c0=c0, piece=piece: contrast(g, c0, piece))
                        after(step + n + 1, lambda g=g, c0=c0, piece=piece: quantise_h(g, c0, piece))
                    if g == 1:
                        product = last_features if j0 + width == S else features
                        after(step + width // piece, lambda product=product, j0=j0, width=width: product(j0, width))
            if 0 <= step - 1 < len(units):
                inverse_root(step - 1)
            for work in later.get(step, []):
                work()
